import numpy as np, ml_dtypes
CORES = [49,52,55,57,60,63,65,68,71,73,76,79]
N = 12
import mx_ref
NC, KT = 128, 1
BF = ml_dtypes.bfloat16
def setup_inputs(rng):
    def f(*shape):
        return mx_ref.flush((rng.standard_normal(shape, dtype=np.float32) * np.exp2(rng.integers(-2, 3, shape[:-1] + (1,)))).astype(BF))
    return {"w": f(N, 128, KT * 512), "x": f(N, 128, KT * 4 * NC)}
def setup_inputs_blocks(rng):
    d = setup_inputs(rng)
    for k in ("w", "x"): d[k] = mx_ref.spread(d[k], rng, 4)
    return d
def setup_inputs_wide(rng):
    d = setup_inputs(rng)
    for k in ("w", "x"): d[k] = mx_ref.flush((d[k].astype(np.float32) * np.exp2(rng.integers(-8, 9, (N, 1, 1))).astype(np.float32)).astype(BF))
    return d
def setup_inputs_zeros(rng):
    d = setup_inputs(rng); v = d["x"].reshape(N, 128, -1, 4).copy()
    v[np.broadcast_to((rng.random((N, 1, v.shape[2], 1)) < 0.33), v.shape)] = 0
    d["x"] = v.reshape(d["x"].shape)
    return d
def reference(w, x):
    QW = [[mx_ref.quantize(w[r][:, 512 * t:512 * t + 512]) for t in range(KT)] for r in range(N)]
    QX = [[mx_ref.quantize(x[j][:, 4 * NC * t:4 * NC * t + 4 * NC]) for t in range(KT)] for j in range(N)]
    y = np.zeros((N, 128, N * NC), np.float32)
    for r in range(N):
        for j in range(N):
            for t in range(KT):
                p = mx_ref.matmul(QW[r][t], QX[j][t])
                y[r][:, NC * j:NC * j + NC] = p if t == 0 else y[r][:, NC * j:NC * j + NC] + p
    return {"y": y}

from concourse.bass import DstId, RemoteDMATransfer
from concourse.mybir import dt, ActivationFunctionType

N = 12
NC = 128
NG = 4

SCRATCH = {
    "xb": ("sbuf", [128, 4 * NC], "bfloat16"),
    "wb": ("sbuf", [128, 4 * NC], "bfloat16"),
    "wq": ("sbuf", [128, NC], "float8_e4m3fn_x4"),
    "ws": ("sbuf", [128, NC], "uint8"),
    "xq": ("sbuf", [128, N * NC], "float8_e4m3fn_x4"),
    "xs": ("sbuf", [128, N * NC], "uint8"),
    "yb": ("sbuf", [128, N * NC], "float32"),
    "ps": ("psum", [128, 512 * NG], "float32"),
}
SEMAPHORES = (["ldx", "ldw", "qx", "qw", "sent", "sta", "stb"]
              + ["c%d" % i for i in range(NG)] + ["p%d" % i for i in range(NG)]
              + ["mm%d" % i for i in range(NG)] + ["cp%d" % i for i in range(NG)])


def _bits(m):
    return [e for e in range(m.bit_length()) if (m >> e) & 1]


def _plan(cores, topo):
    chips = []
    for c in cores:
        if topo.chip(c) not in chips:
            chips.append(topo.chip(c))
    mem = {ch: [c for c in cores if topo.chip(c) == ch] for ch in chips}
    span = {ch: (cores.index(mem[ch][0]), cores.index(mem[ch][-1]) + 1) for ch in chips}
    gi = {ch: i for i, ch in enumerate(chips)}
    role = {}
    for ch in chips:
        mate = [o for o in chips if topo.mates(ch, o)][0]
        plane = [o for o in chips if topo.same_plane(ch, o)][0]
        diag = [o for o in chips if o not in (ch, mate, plane)][0]
        gate = [c for c in mem[ch] if topo.may_write(c, mem[mate][0])][0]
        rest = [c for c in mem[ch] if c != gate]
        far = [c for c in rest if topo.die(c) != topo.die(gate)]
        lp = far[0] if far else rest[0]
        lm = [c for c in rest if c != lp][0]
        role[ch] = {"mate": mate, "plane": plane, "diag": diag, "gate": gate,
                    "lands": {plane: lp, mate: lm, diag: gate}}
    prog = {c: [] for c in cores}
    expect = {}
    sent = {c: 0 for c in cores}

    def send(src, kind, ch, lo, hi, dests):
        prog[src].append(("send", kind, gi[ch], lo, hi, dests))
        for dst, eng in dests:
            key = (dst, "%s%d" % (kind, gi[ch]))
            expect[key] = expect.get(key, 0) + len(eng)
            sent[src] += len(eng)

    def wait(core, kind, ch):
        prog[core].append(("wait", "%s%d" % (kind, gi[ch])))

    for ch in chips:
        r = role[ch]
        over = role[r["plane"]]["lands"][ch]
        for c in mem[ch]:
            j = cores.index(c)
            off = _bits(topo.mask(c, over))
            if c == r["gate"]:
                a, b = [o for o in mem[ch] if o != c]
                on = [e for e in _bits(topo.mask(c, a)) if e not in off]
                d = [(over, off), (a, on[0::2]), (b, on[1::2])]
                send(c, "c", ch, j, j + 1, d)
                send(c, "p", ch, j, j + 1, d)
            else:
                other = [o for o in mem[ch] if o not in (c, r["gate"])][0]
                every = _bits(topo.mask(c, r["gate"]))
                first, second = every[0::2], every[1::2]
                out = [e for e in second if e in off]
                stay = [e for e in second if e not in off]
                send(c, "c", ch, j, j + 1, [(r["gate"], first)])
                send(c, "c", ch, j, j + 1, [(over, out), (other, stay)])
                send(c, "p", ch, j, j + 1, [(r["gate"], first), (over, out), (other, stay)])
    for ch in chips:
        r = role[ch]
        gt = r["gate"]
        lo, hi = span[ch]
        for kind in ("c", "p"):
            wait(gt, kind, ch)
            for to in (r["diag"], r["mate"]):
                dst = role[to]["lands"][ch]
                send(gt, kind, ch, lo, hi, [(dst, _bits(topo.mask(gt, dst)))])
    for ch in chips:
        for src_chip, c in role[ch]["lands"].items():
            lo, hi = span[src_chip]
            a, b = [o for o in mem[ch] if o != c]
            ea, eb = _bits(topo.mask(c, a))[0::2], _bits(topo.mask(c, b))[1::2]
            for kind in ("c", "p"):
                wait(c, kind, src_chip)
                send(c, kind, src_chip, lo, hi, [(a, ea), (b, eb)])
    return chips, span, gi, role, prog, expect, sent


def rank_program(g, core, T, topo):
    if T.rank_of(core) is None:
        return
    cores = list(T.cores)
    me = T.rank_of(core)
    chips, span, gi, role, prog, expect, sent = _plan(cores, topo)
    home = topo.chip(core)
    r = role[home]
    S = T.sem

    g.sync.dma_start(T.xb[:], T.x[:]).then_inc(S.ldx, 16)
    g.scalar.dma_start(T.wb[:], T.w[:]).then_inc(S.ldw, 16)
    g.vector.wait_ge(S.ldx, 16)
    g.vector.quantize_mx(T.xq[:, me * NC:(me + 1) * NC], T.xs[:, me * NC:(me + 1) * NC], T.xb[:]).then_inc(S.qx, 1)
    g.vector.wait_ge(S.ldw, 16)
    g.vector.quantize_mx(T.wq[:], T.ws[:], T.wb[:]).then_inc(S.qw, 1)

    g.wait_ge(S.qx, 1)
    for step in prog[core]:
        if step[0] == "wait":
            g.wait_ge(S[step[1]], expect[(core, step[1])])
            continue
        _, kind, grp, lo, hi, dests = step
        if kind == "c":
            ap = T.xq[:, lo * NC:hi * NC].bitcast(dt.uint8)
        else:
            ap = T.xs[:, lo * NC:hi * NC]
        trs = []
        for dst, eng in dests:
            rid, pid, _se = topo.addr(dst)
            trs.append(RemoteDMATransfer(dst_ids=[DstId(rid=rid, pnc=pid)],
                                         dma_engine_mask=sum(1 << e for e in eng),
                                         remote_sem=S["%s%d" % (kind, grp)], src=ap, dst=ap))
        g.remote_dma_fused(trs, local_sem=S.sent)
    g.wait_ge(S.sent, sent[core])

    if r["lands"][r["mate"]] == core:
        order = [home, r["plane"], r["mate"], r["diag"]]
    else:
        order = [home, r["plane"], r["diag"], r["mate"]]
    g.tensor.wait_ge(S.qw, 1)
    g.tensor.wait_ge(S.qx, 1)
    na = nb = 0
    for i, ch in enumerate(order):
        k = gi[ch]
        lo, hi = span[ch]
        w = (hi - lo) * NC
        for kind in ("c", "p"):
            name = "%s%d" % (kind, k)
            g.tensor.wait_ge(S[name], expect[(core, name)])
        bank = T.ps[:, 512 * i:512 * i + w]
        g.tensor.matmul_mx(bank, T.wq[:], T.ws[:], T.xq[:, lo * NC:hi * NC], T.xs[:, lo * NC:hi * NC],
                           True, True).then_inc(S["mm%d" % i], 1)
        ysb = T.yb[:, lo * NC:hi * NC]
        if i % 2 == 0:
            g.vector.wait_ge(S["mm%d" % i], 1)
            g.vector.tensor_copy(ysb, bank).then_inc(S["cp%d" % i], 1)
            g.sync.wait_ge(S["cp%d" % i], 1)
            g.sync.dma_start(T.y[:, lo * NC:hi * NC], ysb).then_inc(S.sta, 16)
            na += 16
        else:
            g.scalar.wait_ge(S["mm%d" % i], 1)
            g.scalar.activation(ysb, bank, ActivationFunctionType.Copy).then_inc(S["cp%d" % i], 1)
            g.scalar.wait_ge(S["cp%d" % i], 1)
            g.scalar.dma_start(T.y[:, lo * NC:hi * NC], ysb).then_inc(S.stb, 16)
            nb += 16
    g.sync.wait_ge(S.sta, na)
    g.scalar.wait_ge(S.stb, nb)
